import numpy as np
import ml_dtypes


def mxq(x, axis, fmt="e4m3"):
    dtype, down = {"e4m3": (ml_dtypes.float8_e4m3fn, 7), "e5m2": (ml_dtypes.float8_e5m2, 14)}[fmt]
    v = np.moveaxis(np.asarray(x, np.float32).astype(ml_dtypes.bfloat16).astype(np.float64), axis, -1)
    blocks = v.reshape(v.shape[:-1] + (-1, 32))
    amax = np.abs(blocks).max(-1, keepdims=True)
    byte = np.maximum(np.where(amax > 0, np.frexp(amax)[1] - 1 + 127, 0) - down, 1)
    scale = np.exp2(byte - 127.0)
    codes = (blocks / scale).astype(np.float32).astype(dtype).astype(np.float64)
    return np.moveaxis((codes * scale).reshape(v.shape), -1, axis)


WIDE = False


def mx_kscale(k):
    if not WIDE:
        return np.ones(k)
    levels = np.array([10, -10, 5, -5, 0])
    if k % 512:
        return np.exp2(np.random.permutation(np.resize(levels, k // 32))).repeat(32)
    a = np.empty((k // 512, 16))
    for p in range(k // 512):
        a[p, :8] = np.random.permutation(np.resize(levels, 8))
        for g in range(8):
            far = levels[np.abs(levels - a[p, g]) >= 10]
            a[p, g + 8] = far[np.random.randint(len(far))]
    return np.exp2(a.ravel()).repeat(32)


def f64(x):
    return np.asarray(x).astype(np.float64)


def striped(idx):
    return np.tile(idx.reshape(-1, 16).T, (8, 1)).astype(np.uint16)


def unstriped(offs):
    return offs[:16].T.reshape(-1).astype(np.int64)


def striped8(idx):
    return np.concatenate([x.reshape(-1, 16).T for x in idx]).astype(np.uint16)


def runs(offs, k):
    lists = np.stack([offs[16 * r : 16 * r + 16].T.reshape(-1) for r in range(8)]).astype(np.int64)
    return lists[np.arange(k) % 512 // 64]


def pack_weight(w):
    k, n = w.shape
    w = f64(np.asarray(w, np.float32).astype(ml_dtypes.bfloat16)).reshape(k // 32, 32, n)
    amax = np.abs(w).max(1)
    byte = np.clip(np.where(amax > 0, np.frexp(amax)[1] - 1 + 127 - 7, 1), 1, 254)
    scaled = (w * np.exp2(127.0 - byte)[:, None, :]).reshape(k, n).astype(np.float32)
    words = np.ascontiguousarray(scaled.reshape(k // 512, 128, 4, n).transpose(0, 1, 3, 2)).astype(ml_dtypes.float8_e4m3fn).view(np.uint8)
    return words, np.ascontiguousarray(byte.astype(np.uint8).reshape(k // 512, 16, n))


def unpack_weight(words, scales):
    g, p, n, _ = words.shape
    vals = np.ascontiguousarray(words).view(ml_dtypes.float8_e4m3fn).astype(np.float64) * np.repeat(np.exp2(scales.astype(np.float64) - 127.0), 8, axis=1)[..., None]
    return vals.transpose(0, 1, 3, 2).reshape(g * 512, n)


def sigmoid(v):
    return 1.0 / (1.0 + np.exp(-np.maximum(v, -700.0)))


K, T, S, N, G, H = 512, 1024, 512, 512, 2048, 512


def setup_inputs():
    n = np.random.standard_normal
    s = mx_kscale(K)[:, None]
    u = mx_kscale(S)
    packed_xT = pack_weight(n((K, T)) * s)
    packed_dT = pack_weight(n((K, G)) / s)
    return {
        "x_words": packed_xT[0],
        "x_scales": packed_xT[1],
        "d_words": packed_dT[0],
        "d_scales": packed_dT[1],
        "gn": (np.random.uniform(0.5, 1.5, (H, 1)) * u[:, None]).astype(np.float32),
        "gm": (np.random.uniform(0.5, 1.5, (H, 1)) * u[:, None]).astype(np.float32),
        "w1": (n((H, N)) / np.sqrt(2 * H) / u[:, None]).astype(np.float32),
        "w2": (n((H, N)) / np.sqrt(2 * H) / u[:, None]).astype(np.float32),
        "sl": np.random.uniform(1.0, 2.0, (N, 1)).astype(np.float32),
        "th": (0.5 * n((N, 1))).astype(np.float32),
        "offs": striped(np.random.permutation(T)[:S]),
        "k1": striped8(np.random.randint(0, G, (8, H))),
        "two": striped(np.random.permutation(T)[:S]),
        "k2": striped8(np.random.randint(0, G, (8, H))),
        "n1": striped(np.random.randint(0, S, G)),
        "n2": striped8(np.stack([np.random.permutation(S) for _ in range(8)])),
        "n3": striped8(np.stack([np.random.permutation(S) for _ in range(8)])),
        "n4": striped8(np.stack([np.random.permutation(S) for _ in range(8)])),
        "n5": striped8(np.stack([np.random.permutation(S) for _ in range(8)])),
    }


def reference(x_words, x_scales, d_words, d_scales, gn, gm, w1, w2, sl, th, offs, k1, two, k2, n1, n2, n3, n4, n5):
    d_k1 = unpack_weight(d_words, d_scales)[np.arange(K)[:, None], runs(k1, K)]
    xq = unpack_weight(x_words, x_scales)[:, unstriped(offs)]
    a = 0.0625 * (d_k1.T @ xq)
    mb = a[:, unstriped(n1)]
    mn = mb.reshape(H, S, 4).min(axis=2)
    mx = mb.reshape(H, S, 4).max(axis=2)
    z = f64(gn) * (np.maximum(a, mn) - (0.5 * mx))
    d_k2 = unpack_weight(d_words, d_scales)[np.arange(K)[:, None], runs(k2, K)]
    x_two = unpack_weight(x_words, x_scales)[:, unstriped(two)]
    b = 0.0625 * (d_k2.T @ x_two)
    st = b - (b[np.arange(H)[:, None], runs(n2, H)])
    z2 = f64(gm) * (np.maximum(st, st[np.arange(H)[:, None], runs(n3, H)]))
    h = mxq(f64(w1), 0, "e4m3").T @ mxq(z, 0, "e4m3") + mxq(f64(w2), 0, "e4m3").T @ mxq(z2, 0, "e4m3")
    st2 = h - (h[np.arange(N)[:, None], runs(n4, N)])
    sg = sigmoid(f64(sl) * (st2[np.arange(N)[:, None], runs(n5, N)] - f64(th)))
    return h * sg

@@ -1,0 +1,250 @@
+from contextlib import ExitStack
+
+import concourse.mybir as mybir
+
+F32 = mybir.dt.float32
+BF16 = mybir.dt.bfloat16
+I32 = mybir.dt.int32
+U32 = mybir.dt.uint32
+U16 = mybir.dt.uint16
+U8 = mybir.dt.uint8
+FP8X4 = mybir.dt.float8_e4m3fn_x4
+ALU = mybir.AluOpType
+ACT = mybir.ActivationFunctionType
+
+P = 128
+T = 1024
+G = 2048
+S = 512
+PACK = 4
+PIECE = 1024
+FLOPS = 4 * 2 * 512 * 512 * 512
+
+
+def tile_picked_pqjgmidhopmxehq_none_p_kernel(
+    tc, x_words, x_scales, d_words, d_scales, gn, gm, w1, w2, sl, th, offs, k1, two, k2, n1, n2, n3, n4, n5, out
+):
+    nc = tc.nc
+    with ExitStack() as ctx:
+        keep = ctx.enter_context(tc.tile_pool(name="keep", bufs=1))
+        ring = ctx.enter_context(tc.tile_pool(name="ring", bufs=2))
+        laid = ctx.enter_context(tc.tile_pool(name="laid", bufs=1))
+        psum = ctx.enter_context(tc.psum_pool(name="psum", bufs=1))
+
+        def load_list(src, name):
+            tile = keep.tile([P, src.shape[1]], U16, name=name)
+            nc.sync.dma_start(tile[:], src)
+            return tile
+
+        def load_words(src, width, name):
+            tile = keep.tile([P, width], U32, name=name, align_bytes=64)
+            nc.sync.dma_start(tile[:].bitcast(I32), src[0].rearrange("p n t -> p (n t)").bitcast(I32))
+            return tile
+
+        def load_column(src, name):
+            tile = keep.tile([P, PACK], F32, name=name)
+            nc.gpsimd.dma_start(tile[:], src.rearrange("(p t) o -> p (t o)", t=PACK))
+            return tile
+
+        def load_weight(src, name, tag):
+            tile = keep.tile([P, PACK, S], F32, name=name, tag=tag, align_bytes=64)
+            nc.sync.dma_start(tile[:], src.rearrange("(p j) c -> p j c", j=PACK))
+            return tile
+
+        k1_t = load_list(k1, "k1_t")
+        d_bytes = keep.tile([P, G], U8, align_bytes=64)
+        nc.sync.dma_start(
+            d_bytes[:].bitcast(I32), d_scales[0].bitcast(I32).unsqueeze(1).to_broadcast([16, 8, G // 4])
+        )
+        offs_t = load_list(offs, "offs_t")
+        x_bytes = keep.tile([P, T], U8, align_bytes=64)
+        for q in range(4):
+            nc.sync.dma_start(
+                x_bytes[32 * q : 32 * (q + 1), :].bitcast(I32),
+                x_scales[0, 4 * q : 4 * (q + 1), :].bitcast(I32).unsqueeze(0).to_broadcast([8, 4, T // 4]),
+            )
+        x_table = load_words(x_words, T, "x_table")
+        k2_t = load_list(k2, "k2_t")
+        two_t = load_list(two, "two_t")
+        n1_t = load_list(n1, "n1_t")
+        d_table = load_words(d_words, G, "d_table")
+        n2_t = load_list(n2, "n2_t")
+        n3_t = load_list(n3, "n3_t")
+        n4_t = load_list(n4, "n4_t")
+        n5_t = load_list(n5, "n5_t")
+        gn_t = load_column(gn, "gn_t")
+        gm_t = load_column(gm, "gm_t")
+        sl_t = load_column(sl, "sl_t")
+        th_t = load_column(th, "th_t")
+
+        def first_product(d_list, x_list, name, queue, ds, xs, dw, xw):
+            nc.vector.tensor_copy(ds[:], d_bytes[:].indirect(d_list[:]))
+            ds_dealt = keep.tile([P, S], U8, name=name + "_ds_dealt", align_bytes=64)
+            nc.vector.tensor_copy(
+                ds_dealt[:].rearrange("p (t m) -> p m t", t=PACK), ds[:].rearrange("p (m t) -> p m t", t=PACK)
+            )
+            for c in range(1, 4):
+                queue.dma_start(ds_dealt[c:P:32, :].bitcast(I32), ds_dealt[8 * c : P : 32, :].bitcast(I32))
+            nc.vector.tensor_copy(xs[:], x_bytes[:].indirect(x_list[:]))
+            nc.vector.tensor_copy(xw[:], x_table[:].indirect(x_list[:]))
+            nc.vector.tensor_copy(dw[:], d_table[:].indirect(d_list[:]))
+            dw_dealt = keep.tile([P, S], U32, name=name + "_dw_dealt", align_bytes=64)
+            nc.vector.tensor_copy(
+                dw_dealt[:].rearrange("p (t m) -> p m t", t=PACK), dw[:].rearrange("p (m t) -> p m t", t=PACK)
+            )
+            banks = []
+            for t in range(PACK):
+                bank = psum.tile([P, S], F32, name=name + "_bank%d" % t, tag=name + "_bank%d" % t)
+                cols = slice(t * P, (t + 1) * P)
+                nc.tensor.matmul_mx(
+                    out=bank[:],
+                    lhsT=dw_dealt[:, cols].bitcast(FP8X4),
+                    lhsT_scale=ds_dealt[:, cols],
+                    rhs=xw[:].bitcast(FP8X4),
+                    rhs_scale=xs[:],
+                    start=True,
+                    stop=True,
+                )
+                banks.append(bank)
+            return banks
+
+        def quantise(grouped, name):
+            codes = keep.tile([P, S], U32, name=name + "_codes", align_bytes=64)
+            scales = keep.tile([P, S], U8, name=name + "_scales", align_bytes=64)
+            nc.vector.quantize_mx(out=codes[:].bitcast(FP8X4), scales=scales[:], in_=grouped[:])
+            return codes, scales
+
+        def round_weight(raw, name):
+            grouped = keep.tile([P, PACK * S], BF16, name=name + "_grouped", align_bytes=64)
+            nc.gpsimd.tensor_copy(
+                grouped[:].rearrange("p (t m j) -> p t m j", t=PACK, j=PACK),
+                raw[:].rearrange("p j (m t) -> p t m j", t=PACK),
+            )
+            return grouped
+
+        def gain_and_round(values, gain, name):
+            grouped = keep.tile([P, PACK * S], BF16, name=name + "_grouped", align_bytes=64)
+            nc.vector.tensor_tensor(
+                grouped[:].rearrange("p (c i t) -> p c t i", i=4, t=PACK),
+                values[:].rearrange("p t (c i) -> p c t i", i=4),
+                gain[:].unsqueeze(1).unsqueeze(3).to_broadcast([P, S // 4, PACK, 4]),
+                ALU.mult,
+            )
+            return grouped
+
+        a_ds = keep.tile([P, S], U8, tag="a_ds", align_bytes=64)
+        a_xs = keep.tile([P, S], U8, tag="a_xs", align_bytes=64)
+        a_dw = laid.tile([P, S], U32, offset=1536, align_bytes=64)
+        a_xw = keep.tile([P, S], U32, tag="a_xw", align_bytes=64)
+        a_banks = first_product(k1_t, offs_t, "a", nc.sync, a_ds, a_xs, a_dw, a_xw)
+        w1_raw = load_weight(w1, "w1_raw", "a_xs")
+        w2_raw = load_weight(w2, "w2_raw", "a_xw")
+        b_xw = laid.tile([P, S], U32, offset=0, align_bytes=64)
+        b_ds = laid.tile([P, S], U8, offset=2048, align_bytes=64)
+        b_xs = laid.tile([P, S], U8, offset=2560, align_bytes=64)
+        b_dw = laid.tile([P, S], U32, offset=3072, align_bytes=64)
+        b_banks = first_product(k2_t, two_t, "b", nc.sync, b_ds, b_xs, b_dw, b_xw)
+
+        bias_t = keep.tile([P, PACK], F32)
+        minus_sl = keep.tile([P, PACK], F32)
+        nc.gpsimd.tensor_scalar(minus_sl[:], sl_t[:], -1.0, 0.0, ALU.mult, ALU.add)
+        nc.gpsimd.tensor_tensor(bias_t[:], minus_sl[:], th_t[:], ALU.mult)
+
+        z_raw = keep.tile([P, PACK, S], F32)
+        z2_raw = keep.tile([P, PACK, S], F32)
+        w_grouped = []
+        for t in range(PACK):
+            a_row = keep.tile([P, PIECE + 32], F32, name="a_row%d" % t)
+            nc.scalar.activation(a_row[:, :S], a_banks[t][:], ACT.Copy, scale=0.0625)
+            lo = ring.tile([P, S, 2], F32, name="lo")
+            hi = ring.tile([P, S, 2], F32, name="hi")
+            for piece in range(4 * S // PIECE):
+                members = ring.tile([P, PIECE // 4, 4], F32, name="members", bufs=4)
+                nc.scalar.activation(
+                    members[:].rearrange("p j m -> p (j m)"),
+                    a_row[:].indirect(n1_t[:, piece * PIECE // 16 : (piece + 1) * PIECE // 16]),
+                    ACT.Copy,
+                )
+                cols = slice(piece * PIECE // 4, (piece + 1) * PIECE // 4)
+                nc.vector.tensor_tensor(lo[:, cols, :], members[:, :, 0:2], members[:, :, 2:4], ALU.min)
+                nc.vector.tensor_tensor(hi[:, cols, :], members[:, :, 0:2], members[:, :, 2:4], ALU.max)
+            mn = ring.tile([P, S], F32, name="mn")
+            nc.vector.tensor_tensor(mn[:], lo[:, :, 0], lo[:, :, 1], ALU.min)
+            mx = ring.tile([P, S], F32, name="mx")
+            nc.vector.tensor_tensor(mx[:], hi[:, :, 0], hi[:, :, 1], ALU.max)
+            up = ring.tile([P, S], F32, name="up")
+            nc.vector.tensor_tensor(up[:], mn[:], a_row[:, :S], ALU.max)
+            nc.vector.scalar_tensor_tensor(z_raw[:, t, :], mx[:], -0.5, up[:], ALU.mult, ALU.add)
+            if t < 2:
+                w_grouped.append(round_weight((w1_raw, w2_raw)[t], "w%d" % (t + 1)))
+        w1_codes, w1_scales = quantise(w_grouped[0], "w1")
+        w2_codes, w2_scales = quantise(w_grouped[1], "w2")
+        z_codes, z_scales = quantise(gain_and_round(z_raw, gn_t, "z"), "z")
+
+        h_banks = []
+        for t in range(PACK):
+            bank = psum.tile([P, S], F32, name="h_bank%d" % t, tag="a_bank%d" % t)
+            cols = slice(t * P, (t + 1) * P)
+            nc.tensor.matmul_mx(
+                out=bank[:],
+                lhsT=w1_codes[:, cols].bitcast(FP8X4),
+                lhsT_scale=w1_scales[:, cols],
+                rhs=z_codes[:].bitcast(FP8X4),
+                rhs_scale=z_scales[:],
+                start=True,
+                stop=False,
+            )
+            h_banks.append(bank)
+
+        for t in range(PACK):
+            b_row = ring.tile([P, 2 * S], F32, name="b_row", tag="first_window", bufs=4)
+            nc.scalar.activation(b_row[:, :S], b_banks[t][:], ACT.Copy, scale=0.0625)
+            b_n2 = ring.tile([P, S], F32, name="b_n2")
+            nc.scalar.activation(b_n2[:], b_row[:].indirect(n2_t[:]), ACT.Copy)
+            st = ring.tile([P, 2 * S], F32, name="st", tag="second_window", bufs=4)
+            nc.vector.tensor_tensor(st[:, :S], b_row[:, :S], b_n2[:], ALU.subtract)
+            st_n3 = ring.tile([P, S], F32, name="st_n3")
+            nc.scalar.activation(st_n3[:], st[:].indirect(n3_t[:]), ACT.Copy)
+            nc.vector.tensor_tensor(z2_raw[:, t, :], st[:, :S], st_n3[:], ALU.max)
+        z2_codes, z2_scales = quantise(gain_and_round(z2_raw, gm_t, "z2"), "z2")
+
+        out_rows = out.rearrange("(p t) j -> t p j", t=PACK)
+        for t in range(PACK):
+            cols = slice(t * P, (t + 1) * P)
+            nc.tensor.matmul_mx(
+                out=h_banks[t][:],
+                lhsT=w2_codes[:, cols].bitcast(FP8X4),
+                lhsT_scale=w2_scales[:, cols],
+                rhs=z2_codes[:].bitcast(FP8X4),
+                rhs_scale=z2_scales[:],
+                start=False,
+                stop=True,
+            )
+        h_rows = []
+        for t in range(PACK):
+            h_row = ring.tile([P, 2 * S], F32, name="h_row", tag="first_window", bufs=4)
+            if t == 0:
+                nc.vector.tensor_copy(h_row[:, :S], h_banks[t][:])
+            else:
+                nc.scalar.copy(h_row[:, :S], h_banks[t][:])
+            h_rows.append(h_row)
+        h_n4_last = ring.tile([P, S], F32, name="h_n4_last", bufs=1)
+        nc.scalar.activation(h_n4_last[:], h_rows[PACK - 1][:].indirect(n4_t[:]), ACT.Copy)
+        st2s = []
+        for t in range(PACK):
+            if t < PACK - 1:
+                h_n4 = ring.tile([P, S], F32, name="h_n4")
+                nc.vector.tensor_copy(h_n4[:], h_rows[t][:].indirect(n4_t[:]))
+            else:
+                h_n4 = h_n4_last
+            st2 = ring.tile([P, 2 * S], F32, name="st2", tag="second_window", bufs=4)
+            nc.vector.tensor_tensor(st2[:, :S], h_banks[t][:], h_n4[:], ALU.subtract)
+            st2s.append(st2)
+        for t in range(PACK):
+            sg = ring.tile([P, S], F32, name="sg", bufs=4)
+            nc.scalar.activation(
+                sg[:], st2s[t][:].indirect(n5_t[:]), ACT.Sigmoid, bias=bias_t[:, t : t + 1], scale=sl_t[:, t : t + 1]
+            )
+            res = ring.tile([P, S], F32, name="res", bufs=4)
+            nc.vector.tensor_tensor(res[:], h_banks[t][:], sg[:], ALU.mult)
+            nc.sync.dma_start(out_rows[t], res[:])

@@ -114,11 +114,11 @@ def tile_picked_pqjgmidhopmxehq_none_p_kernel(
             nc.vector.quantize_mx(out=codes[:].bitcast(FP8X4), scales=scales[:], in_=grouped[:])
             return codes, scales
 
-        def round_weight(raw, name):
-            grouped = keep.tile([P, PACK * S], BF16, name=name + "_grouped", align_bytes=64)
-            nc.gpsimd.tensor_copy(
-                grouped[:].rearrange("p (t m j) -> p t m j", t=PACK, j=PACK),
-                raw[:].rearrange("p j (m t) -> p t m j", t=PACK),
+        def round_weight(raw, name, tag):
+            grouped = keep.tile([P, PACK * S], BF16, name=name + "_grouped", tag=tag, align_bytes=64)
+            nc.scalar.copy(
+                grouped[:].rearrange("p (t m j) -> p m j t", t=PACK, j=PACK),
+                raw[:].rearrange("p j (m t) -> p m j t", t=PACK),
             )
             return grouped
 
@@ -152,14 +152,18 @@ def tile_picked_pqjgmidhopmxehq_none_p_kernel(
 
         z_raw = keep.tile([P, PACK, S], F32)
         z2_raw = keep.tile([P, PACK, S], F32)
-        w_grouped = []
+
+        def finish_z(t, mx, up):
+            nc.vector.scalar_tensor_tensor(z_raw[:, t, :], mx[:], -0.5, up[:], ALU.mult, ALU.add)
+
+        pending = None
         for t in range(PACK):
             a_row = keep.tile([P, PIECE + 32], F32, name="a_row%d" % t)
             nc.scalar.activation(a_row[:, :S], a_banks[t][:], ACT.Copy, scale=0.0625)
             lo = ring.tile([P, S, 2], F32, name="lo")
             hi = ring.tile([P, S, 2], F32, name="hi")
             for piece in range(4 * S // PIECE):
-                members = ring.tile([P, PIECE // 4, 4], F32, name="members", bufs=4)
+                members = ring.tile([P, PIECE // 4, 4], F32, name="members", tag="members", bufs=8)
                 nc.scalar.activation(
                     members[:].rearrange("p j m -> p (j m)"),
                     a_row[:].indirect(n1_t[:, piece * PIECE // 16 : (piece + 1) * PIECE // 16]),
@@ -167,6 +171,8 @@ def tile_picked_pqjgmidhopmxehq_none_p_kernel(
                 )
                 cols = slice(piece * PIECE // 4, (piece + 1) * PIECE // 4)
                 nc.vector.tensor_tensor(lo[:, cols, :], members[:, :, 0:2], members[:, :, 2:4], ALU.min)
+                if piece == 0 and pending is not None:
+                    finish_z(*pending)
                 nc.vector.tensor_tensor(hi[:, cols, :], members[:, :, 0:2], members[:, :, 2:4], ALU.max)
             mn = ring.tile([P, S], F32, name="mn")
             nc.vector.tensor_tensor(mn[:], lo[:, :, 0], lo[:, :, 1], ALU.min)
@@ -174,77 +180,96 @@ def tile_picked_pqjgmidhopmxehq_none_p_kernel(
             nc.vector.tensor_tensor(mx[:], hi[:, :, 0], hi[:, :, 1], ALU.max)
             up = ring.tile([P, S], F32, name="up")
             nc.vector.tensor_tensor(up[:], mn[:], a_row[:, :S], ALU.max)
-            nc.vector.scalar_tensor_tensor(z_raw[:, t, :], mx[:], -0.5, up[:], ALU.mult, ALU.add)
-            if t < 2:
-                w_grouped.append(round_weight((w1_raw, w2_raw)[t], "w%d" % (t + 1)))
-        w1_codes, w1_scales = quantise(w_grouped[0], "w1")
-        w2_codes, w2_scales = quantise(w_grouped[1], "w2")
-        z_codes, z_scales = quantise(gain_and_round(z_raw, gn_t, "z"), "z")
+            pending = (t, mx, up)
 
-        h_banks = []
+        b_rows, b_n2s, sts = [], [], []
         for t in range(PACK):
-            bank = psum.tile([P, S], F32, name="h_bank%d" % t, tag="a_bank%d" % t)
-            cols = slice(t * P, (t + 1) * P)
-            nc.tensor.matmul_mx(
-                out=bank[:],
-                lhsT=w1_codes[:, cols].bitcast(FP8X4),
-                lhsT_scale=w1_scales[:, cols],
-                rhs=z_codes[:].bitcast(FP8X4),
-                rhs_scale=z_scales[:],
-                start=True,
-                stop=False,
-            )
-            h_banks.append(bank)
-
-        for t in range(PACK):
-            b_row = ring.tile([P, 2 * S], F32, name="b_row", tag="first_window", bufs=4)
+            b_row = keep.tile([P, 2 * S], F32, name="b_row", tag="first_window%d" % t, align_bytes=64)
             nc.scalar.activation(b_row[:, :S], b_banks[t][:], ACT.Copy, scale=0.0625)
-            b_n2 = ring.tile([P, S], F32, name="b_n2")
+            b_n2 = keep.tile([P, S], F32, name="b_n2", tag="b_n2_%d" % t, align_bytes=64)
             nc.scalar.activation(b_n2[:], b_row[:].indirect(n2_t[:]), ACT.Copy)
-            st = ring.tile([P, 2 * S], F32, name="st", tag="second_window", bufs=4)
-            nc.vector.tensor_tensor(st[:, :S], b_row[:, :S], b_n2[:], ALU.subtract)
-            st_n3 = ring.tile([P, S], F32, name="st_n3")
-            nc.scalar.activation(st_n3[:], st[:].indirect(n3_t[:]), ACT.Copy)
-            nc.vector.tensor_tensor(z2_raw[:, t, :], st[:, :S], st_n3[:], ALU.max)
-        z2_codes, z2_scales = quantise(gain_and_round(z2_raw, gm_t, "z2"), "z2")
+            b_rows.append(b_row)
+            b_n2s.append(b_n2)
+
+        def difference(t):
+            st = keep.tile([P, 2 * S], F32, name="st", tag="second_window%d" % t)
+            nc.vector.tensor_tensor(st[:, :S], b_rows[t][:, :S], b_n2s[t][:], ALU.subtract)
+            sts.append(st)
+
+        difference(0)
+        finish_z(*pending)
+        difference(1)
+        z_grouped = gain_and_round(z_raw, gn_t, "z")
+        difference(2)
+        z_codes, z_scales = quantise(z_grouped, "z")
+        difference(3)
+        for t in range(PACK):
+            st_n3 = ring.tile([P, S], F32, name="st_n3", tag="fetched", bufs=4)
+            nc.scalar.activation(st_n3[:], sts[t][:].indirect(n3_t[:]), ACT.Copy)
+            nc.vector.tensor_tensor(z2_raw[:, t, :], sts[t][:, :S], st_n3[:], ALU.max)
+        w1_grouped = round_weight(w1_raw, "w1", "first_window3")
+        w2_grouped = round_weight(w2_raw, "w2", "b_n2_3")
+        z2_grouped = gain_and_round(z2_raw, gm_t, "z2")
+        w1_codes, w1_scales = quantise(w1_grouped, "w1")
+        z2_codes, z2_scales = quantise(z2_grouped, "z2")
+        w2_codes, w2_scales = quantise(w2_grouped, "w2")
+
+        h_banks = [psum.tile([P, S], F32, name="h_bank%d" % t, tag="a_bank%d" % t) for t in range(PACK)]
+        passes = ((w1_codes, w1_scales, z_codes, z_scales), (w2_codes, w2_scales, z2_codes, z2_scales))
+        for n, (w_codes, w_scales, codes, scales) in enumerate(passes):
+            for t in range(PACK):
+                cols = slice(t * P, (t + 1) * P)
+                nc.tensor.matmul_mx(
+                    out=h_banks[t][:],
+                    lhsT=w_codes[:, cols].bitcast(FP8X4),
+                    lhsT_scale=w_scales[:, cols],
+                    rhs=codes[:].bitcast(FP8X4),
+                    rhs_scale=scales[:],
+                    start=(n == 0),
+                    stop=(n == 1),
+                )
 
         out_rows = out.rearrange("(p t) j -> t p j", t=PACK)
-        for t in range(PACK):
-            cols = slice(t * P, (t + 1) * P)
-            nc.tensor.matmul_mx(
-                out=h_banks[t][:],
-                lhsT=w2_codes[:, cols].bitcast(FP8X4),
-                lhsT_scale=w2_scales[:, cols],
-                rhs=z2_codes[:].bitcast(FP8X4),
-                rhs_scale=z2_scales[:],
-                start=False,
-                stop=True,
-            )
         h_rows = []
         for t in range(PACK):
-            h_row = ring.tile([P, 2 * S], F32, name="h_row", tag="first_window", bufs=4)
+            h_row = keep.tile([P, 2 * S], F32, name="h_row%d" % t)
             if t == 0:
                 nc.vector.tensor_copy(h_row[:, :S], h_banks[t][:])
             else:
                 nc.scalar.copy(h_row[:, :S], h_banks[t][:])
             h_rows.append(h_row)
-        h_n4_last = ring.tile([P, S], F32, name="h_n4_last", bufs=1)
-        nc.scalar.activation(h_n4_last[:], h_rows[PACK - 1][:].indirect(n4_t[:]), ACT.Copy)
+        h_n4s = [ring.tile([P, S], F32, name="h_n4", tag="fetched", bufs=4) for t in range(PACK)]
         st2s = []
-        for t in range(PACK):
-            if t < PACK - 1:
-                h_n4 = ring.tile([P, S], F32, name="h_n4")
-                nc.vector.tensor_copy(h_n4[:], h_rows[t][:].indirect(n4_t[:]))
-            else:
-                h_n4 = h_n4_last
-            st2 = ring.tile([P, 2 * S], F32, name="st2", tag="second_window", bufs=4)
-            nc.vector.tensor_tensor(st2[:, :S], h_banks[t][:], h_n4[:], ALU.subtract)
+
+        def fetch_h(t):
+            nc.vector.tensor_copy(h_n4s[t][:], h_rows[t][:].indirect(n4_t[:]))
+
+        def second_difference(t):
+            st2 = keep.tile([P, 2 * S], F32, name="st2", tag="second_window%d" % t)
+            nc.vector.tensor_tensor(st2[:, :S], h_rows[t][:, :S], h_n4s[t][:], ALU.subtract)
             st2s.append(st2)
+
+        nc.scalar.activation(h_n4s[2][:], h_rows[2][:].indirect(n4_t[:]), ACT.Copy)
+        fetch_h(0)
+        fetch_h(1)
+        second_difference(0)
+        second_difference(1)
+        fetch_h(3)
+        second_difference(2)
+        second_difference(3)
         for t in range(PACK):
-            sg = ring.tile([P, S], F32, name="sg", bufs=4)
-            nc.scalar.activation(
-                sg[:], st2s[t][:].indirect(n5_t[:]), ACT.Sigmoid, bias=bias_t[:, t : t + 1], scale=sl_t[:, t : t + 1]
-            )
-            res = ring.tile([P, S], F32, name="res", bufs=4)
-            nc.vector.tensor_tensor(res[:], h_banks[t][:], sg[:], ALU.mult)
-            nc.sync.dma_start(out_rows[t], res[:])
+            halves = 2 if t == PACK - 1 else 1
+            width = S // halves
+            for half in range(halves):
+                cols = slice(half * width, (half + 1) * width)
+                sg = ring.tile([P, width], F32, name="sg", tag="members", bufs=8)
+                nc.scalar.activation(
+                    sg[:],
+                    st2s[t][:].indirect(n5_t[:, half * width // 16 : (half + 1) * width // 16]),
+                    ACT.Sigmoid,
+                    bias=bias_t[:, t : t + 1],
+                    scale=sl_t[:, t : t + 1],
+                )
+                res = ring.tile([P, width], F32, name="res", tag="members", bufs=8)
+                nc.vector.tensor_tensor(res[:], h_rows[t][:, cols], sg[:], ALU.mult)
+                nc.sync.dma_start(out_rows[t][:, cols], res[:])

@@ -77,6 +77,9 @@ def tile_picked_pqjgmidhopmxehq_none_p_kernel(
         sl_t = load_column(sl, "sl_t")
         th_t = load_column(th, "th_t")
 
+        warm = keep.tile([P, 1], F32)
+        nc.scalar.activation(warm[:], gn_t[:, 0:1], ACT.Sigmoid)
+
         def first_product(d_list, x_list, name, queue, ds, xs, dw, xw):
             nc.vector.tensor_copy(ds[:], d_bytes[:].indirect(d_list[:]))
             ds_dealt = keep.tile([P, S], U8, name=name + "_ds_dealt", align_bytes=64)

@@ -63,13 +63,13 @@ def tile_picked_pqjgmidhopmxehq_none_p_kernel(
                 x_bytes[32 * q : 32 * (q + 1), :].bitcast(I32),
                 x_scales[0, 4 * q : 4 * (q + 1), :].bitcast(I32).unsqueeze(0).to_broadcast([8, 4, T // 4]),
             )
+        d_table = load_words(d_words, G, "d_table")
+        n1_t = load_list(n1, "n1_t")
+        n2_t = load_list(n2, "n2_t")
+        n3_t = load_list(n3, "n3_t")
         x_table = load_words(x_words, T, "x_table")
         k2_t = load_list(k2, "k2_t")
         two_t = load_list(two, "two_t")
-        n1_t = load_list(n1, "n1_t")
-        d_table = load_words(d_words, G, "d_table")
-        n2_t = load_list(n2, "n2_t")
-        n3_t = load_list(n3, "n3_t")
         n4_t = load_list(n4, "n4_t")
         n5_t = load_list(n5, "n5_t")
         gn_t = load_column(gn, "gn_t")
@@ -89,8 +89,8 @@ def tile_picked_pqjgmidhopmxehq_none_p_kernel(
             for c in range(1, 4):
                 queue.dma_start(ds_dealt[c:P:32, :].bitcast(I32), ds_dealt[8 * c : P : 32, :].bitcast(I32))
             nc.vector.tensor_copy(xs[:], x_bytes[:].indirect(x_list[:]))
-            nc.vector.tensor_copy(xw[:], x_table[:].indirect(x_list[:]))
             nc.vector.tensor_copy(dw[:], d_table[:].indirect(d_list[:]))
+            nc.vector.tensor_copy(xw[:], x_table[:].indirect(x_list[:]))
             dw_dealt = keep.tile([P, S], U32, name=name + "_dw_dealt", align_bytes=64)
             nc.vector.tensor_copy(
                 dw_dealt[:].rearrange("p (t m) -> p m t", t=PACK), dw[:].rearrange("p (m t) -> p m t", t=PACK)
@@ -249,7 +249,7 @@ def tile_picked_pqjgmidhopmxehq_none_p_kernel(
 
         def second_difference(t):
             st2 = keep.tile([P, 2 * S], F32, name="st2", tag="second_window%d" % t)
-            nc.vector.tensor_tensor(st2[:, :S], h_rows[t][:, :S], h_n4s[t][:], ALU.subtract)
+            nc.vector.tensor_tensor(st2[:, :S], h_banks[t][:], h_n4s[t][:], ALU.subtract)
             st2s.append(st2)
 
         nc.scalar.activation(h_n4s[2][:], h_rows[2][:].indirect(n4_t[:]), ACT.Copy)
@@ -257,8 +257,8 @@ def tile_picked_pqjgmidhopmxehq_none_p_kernel(
         fetch_h(1)
         second_difference(0)
         second_difference(1)
-        fetch_h(3)
         second_difference(2)
+        fetch_h(3)
         second_difference(3)
         for t in range(PACK):
             halves = 2 if t == PACK - 1 else 1
@@ -274,5 +274,8 @@ def tile_picked_pqjgmidhopmxehq_none_p_kernel(
                     scale=sl_t[:, t : t + 1],
                 )
                 res = ring.tile([P, width], F32, name="res", tag="members", bufs=8)
-                nc.vector.tensor_tensor(res[:], h_rows[t][:, cols], sg[:], ALU.mult)
+                if t < 2:
+                    nc.gpsimd.tensor_tensor(res[:], h_rows[t][:, cols], sg[:], ALU.mult)
+                else:
+                    nc.vector.tensor_tensor(res[:], h_banks[t][:, cols], sg[:], ALU.mult)
                 nc.sync.dma_start(out_rows[t][:, cols], res[:])

from contextlib import ExitStack

import concourse.mybir as mybir

F32 = mybir.dt.float32
BF16 = mybir.dt.bfloat16
I32 = mybir.dt.int32
U32 = mybir.dt.uint32
U16 = mybir.dt.uint16
U8 = mybir.dt.uint8
FP8X4 = mybir.dt.float8_e4m3fn_x4
ALU = mybir.AluOpType
ACT = mybir.ActivationFunctionType

P = 128
T = 1024
G = 2048
S = 512
PACK = 4
PIECE = 1024
FLOPS = 4 * 2 * 512 * 512 * 512


def tile_picked_pqjgmidhopmxehq_none_p_kernel(
    tc, x_words, x_scales, d_words, d_scales, gn, gm, w1, w2, sl, th, offs, k1, two, k2, n1, n2, n3, n4, n5, out
):
    nc = tc.nc
    with ExitStack() as ctx:
        keep = ctx.enter_context(tc.tile_pool(name="keep", bufs=1))
        ring = ctx.enter_context(tc.tile_pool(name="ring", bufs=2))
        laid = ctx.enter_context(tc.tile_pool(name="laid", bufs=1))
        psum = ctx.enter_context(tc.psum_pool(name="psum", bufs=1))

        def load_list(src, name):
            tile = keep.tile([P, src.shape[1]], U16, name=name)
            nc.sync.dma_start(tile[:], src)
            return tile

        def load_words(src, width, name):
            tile = keep.tile([P, width], U32, name=name, align_bytes=64)
            nc.sync.dma_start(tile[:].bitcast(I32), src[0].rearrange("p n t -> p (n t)").bitcast(I32))
            return tile

        def load_column(src, name):
            tile = keep.tile([P, PACK], F32, name=name)
            nc.gpsimd.dma_start(tile[:], src.rearrange("(p t) o -> p (t o)", t=PACK))
            return tile

        def load_weight(src, name, tag):
            tile = keep.tile([P, PACK, S], F32, name=name, tag=tag, align_bytes=64)
            nc.sync.dma_start(tile[:], src.rearrange("(p j) c -> p j c", j=PACK))
            return tile

        k1_t = load_list(k1, "k1_t")
        d_bytes = keep.tile([P, G], U8, align_bytes=64)
        nc.sync.dma_start(
            d_bytes[:].bitcast(I32), d_scales[0].bitcast(I32).unsqueeze(1).to_broadcast([16, 8, G // 4])
        )
        offs_t = load_list(offs, "offs_t")
        x_bytes = keep.tile([P, T], U8, align_bytes=64)
        for q in range(4):
            nc.sync.dma_start(
                x_bytes[32 * q : 32 * (q + 1), :].bitcast(I32),
                x_scales[0, 4 * q : 4 * (q + 1), :].bitcast(I32).unsqueeze(0).to_broadcast([8, 4, T // 4]),
            )
        d_table = load_words(d_words, G, "d_table")
        n1_t = load_list(n1, "n1_t")
        n2_t = load_list(n2, "n2_t")
        n3_t = load_list(n3, "n3_t")
        x_table = load_words(x_words, T, "x_table")
        k2_t = load_list(k2, "k2_t")
        two_t = load_list(two, "two_t")
        n4_t = load_list(n4, "n4_t")
        n5_t = load_list(n5, "n5_t")
        gn_t = load_column(gn, "gn_t")
        gm_t = load_column(gm, "gm_t")
        sl_t = load_column(sl, "sl_t")
        th_t = load_column(th, "th_t")

        warm = keep.tile([P, 1], F32)
        nc.scalar.activation(warm[:], gn_t[:, 0:1], ACT.Sigmoid)

        def first_product(d_list, x_list, name, queue, ds, xs, dw, xw):
            nc.vector.tensor_copy(ds[:], d_bytes[:].indirect(d_list[:]))
            ds_dealt = keep.tile([P, S], U8, name=name + "_ds_dealt", align_bytes=64)
            nc.vector.tensor_copy(
                ds_dealt[:].rearrange("p (t m) -> p m t", t=PACK), ds[:].rearrange("p (m t) -> p m t", t=PACK)
            )
            for c in range(1, 4):
                queue.dma_start(ds_dealt[c:P:32, :].bitcast(I32), ds_dealt[8 * c : P : 32, :].bitcast(I32))
            nc.vector.tensor_copy(xs[:], x_bytes[:].indirect(x_list[:]))
            nc.vector.tensor_copy(dw[:], d_table[:].indirect(d_list[:]))
            nc.vector.tensor_copy(xw[:], x_table[:].indirect(x_list[:]))
            dw_dealt = keep.tile([P, S], U32, name=name + "_dw_dealt", align_bytes=64)
            nc.vector.tensor_copy(
                dw_dealt[:].rearrange("p (t m) -> p m t", t=PACK), dw[:].rearrange("p (m t) -> p m t", t=PACK)
            )
            banks = []
            for t in range(PACK):
                bank = psum.tile([P, S], F32, name=name + "_bank%d" % t, tag=name + "_bank%d" % t)
                cols = slice(t * P, (t + 1) * P)
                nc.tensor.matmul_mx(
                    out=bank[:],
                    lhsT=dw_dealt[:, cols].bitcast(FP8X4),
                    lhsT_scale=ds_dealt[:, cols],
                    rhs=xw[:].bitcast(FP8X4),
                    rhs_scale=xs[:],
                    start=True,
                    stop=True,
                )
                banks.append(bank)
            return banks

        def quantise(grouped, name):
            codes = keep.tile([P, S], U32, name=name + "_codes", align_bytes=64)
            scales = keep.tile([P, S], U8, name=name + "_scales", align_bytes=64)
            nc.vector.quantize_mx(out=codes[:].bitcast(FP8X4), scales=scales[:], in_=grouped[:])
            return codes, scales

        def round_weight(raw, name, tag):
            grouped = keep.tile([P, PACK * S], BF16, name=name + "_grouped", tag=tag, align_bytes=64)
            nc.scalar.copy(
                grouped[:].rearrange("p (t m j) -> p m j t", t=PACK, j=PACK),
                raw[:].rearrange("p j (m t) -> p m j t", t=PACK),
            )
            return grouped

        def gain_and_round(values, gain, name):
            grouped = keep.tile([P, PACK * S], BF16, name=name + "_grouped", align_bytes=64)
            nc.vector.tensor_tensor(
                grouped[:].rearrange("p (c i t) -> p c t i", i=4, t=PACK),
                values[:].rearrange("p t (c i) -> p c t i", i=4),
                gain[:].unsqueeze(1).unsqueeze(3).to_broadcast([P, S // 4, PACK, 4]),
                ALU.mult,
            )
            return grouped

        a_ds = keep.tile([P, S], U8, tag="a_ds", align_bytes=64)
        a_xs = keep.tile([P, S], U8, tag="a_xs", align_bytes=64)
        a_dw = laid.tile([P, S], U32, offset=1536, align_bytes=64)
        a_xw = keep.tile([P, S], U32, tag="a_xw", align_bytes=64)
        a_banks = first_product(k1_t, offs_t, "a", nc.sync, a_ds, a_xs, a_dw, a_xw)
        w1_raw = load_weight(w1, "w1_raw", "a_xs")
        w2_raw = load_weight(w2, "w2_raw", "a_xw")
        b_xw = laid.tile([P, S], U32, offset=0, align_bytes=64)
        b_ds = laid.tile([P, S], U8, offset=2048, align_bytes=64)
        b_xs = laid.tile([P, S], U8, offset=2560, align_bytes=64)
        b_dw = laid.tile([P, S], U32, offset=3072, align_bytes=64)
        b_banks = first_product(k2_t, two_t, "b", nc.sync, b_ds, b_xs, b_dw, b_xw)

        bias_t = keep.tile([P, PACK], F32)
        minus_sl = keep.tile([P, PACK], F32)
        nc.gpsimd.tensor_scalar(minus_sl[:], sl_t[:], -1.0, 0.0, ALU.mult, ALU.add)
        nc.gpsimd.tensor_tensor(bias_t[:], minus_sl[:], th_t[:], ALU.mult)

        z_raw = keep.tile([P, PACK, S], F32)
        z2_raw = keep.tile([P, PACK, S], F32)

        def finish_z(t, mx, up):
            nc.vector.scalar_tensor_tensor(z_raw[:, t, :], mx[:], -0.5, up[:], ALU.mult, ALU.add)

        pending = None
        for t in range(PACK):
            a_row = keep.tile([P, PIECE + 32], F32, name="a_row%d" % t)
            nc.scalar.activation(a_row[:, :S], a_banks[t][:], ACT.Copy, scale=0.0625)
            lo = ring.tile([P, S, 2], F32, name="lo")
            hi = ring.tile([P, S, 2], F32, name="hi")
            for piece in range(4 * S // PIECE):
                members = ring.tile([P, PIECE // 4, 4], F32, name="members", tag="members", bufs=8)
                nc.scalar.activation(
                    members[:].rearrange("p j m -> p (j m)"),
                    a_row[:].indirect(n1_t[:, piece * PIECE // 16 : (piece + 1) * PIECE // 16]),
                    ACT.Copy,
                )
                cols = slice(piece * PIECE // 4, (piece + 1) * PIECE // 4)
                nc.vector.tensor_tensor(lo[:, cols, :], members[:, :, 0:2], members[:, :, 2:4], ALU.min)
                if piece == 0 and pending is not None:
                    finish_z(*pending)
                nc.vector.tensor_tensor(hi[:, cols, :], members[:, :, 0:2], members[:, :, 2:4], ALU.max)
            mn = ring.tile([P, S], F32, name="mn")
            nc.vector.tensor_tensor(mn[:], lo[:, :, 0], lo[:, :, 1], ALU.min)
            mx = ring.tile([P, S], F32, name="mx")
            nc.vector.tensor_tensor(mx[:], hi[:, :, 0], hi[:, :, 1], ALU.max)
            up = ring.tile([P, S], F32, name="up")
            nc.vector.tensor_tensor(up[:], mn[:], a_row[:, :S], ALU.max)
            pending = (t, mx, up)

        b_rows, b_n2s, sts = [], [], []
        for t in range(PACK):
            b_row = keep.tile([P, 2 * S], F32, name="b_row", tag="first_window%d" % t, align_bytes=64)
            nc.scalar.activation(b_row[:, :S], b_banks[t][:], ACT.Copy, scale=0.0625)
            b_n2 = keep.tile([P, S], F32, name="b_n2", tag="b_n2_%d" % t, align_bytes=64)
            nc.scalar.activation(b_n2[:], b_row[:].indirect(n2_t[:]), ACT.Copy)
            b_rows.append(b_row)
            b_n2s.append(b_n2)

        def difference(t):
            st = keep.tile([P, 2 * S], F32, name="st", tag="second_window%d" % t)
            nc.vector.tensor_tensor(st[:, :S], b_rows[t][:, :S], b_n2s[t][:], ALU.subtract)
            sts.append(st)

        difference(0)
        finish_z(*pending)
        difference(1)
        z_grouped = gain_and_round(z_raw, gn_t, "z")
        difference(2)
        z_codes, z_scales = quantise(z_grouped, "z")
        difference(3)
        for t in range(PACK):
            st_n3 = ring.tile([P, S], F32, name="st_n3", tag="fetched", bufs=4)
            nc.scalar.activation(st_n3[:], sts[t][:].indirect(n3_t[:]), ACT.Copy)
            nc.vector.tensor_tensor(z2_raw[:, t, :], sts[t][:, :S], st_n3[:], ALU.max)
        w1_grouped = round_weight(w1_raw, "w1", "first_window3")
        w2_grouped = round_weight(w2_raw, "w2", "b_n2_3")
        z2_grouped = gain_and_round(z2_raw, gm_t, "z2")
        w1_codes, w1_scales = quantise(w1_grouped, "w1")
        z2_codes, z2_scales = quantise(z2_grouped, "z2")
        w2_codes, w2_scales = quantise(w2_grouped, "w2")

        h_banks = [psum.tile([P, S], F32, name="h_bank%d" % t, tag="a_bank%d" % t) for t in range(PACK)]
        passes = ((w1_codes, w1_scales, z_codes, z_scales), (w2_codes, w2_scales, z2_codes, z2_scales))
        for n, (w_codes, w_scales, codes, scales) in enumerate(passes):
            for t in range(PACK):
                cols = slice(t * P, (t + 1) * P)
                nc.tensor.matmul_mx(
                    out=h_banks[t][:],
                    lhsT=w_codes[:, cols].bitcast(FP8X4),
                    lhsT_scale=w_scales[:, cols],
                    rhs=codes[:].bitcast(FP8X4),
                    rhs_scale=scales[:],
                    start=(n == 0),
                    stop=(n == 1),
                )

        out_rows = out.rearrange("(p t) j -> t p j", t=PACK)
        h_rows = []
        for t in range(PACK):
            h_row = keep.tile([P, 2 * S], F32, name="h_row%d" % t)
            if t == 0:
                nc.vector.tensor_copy(h_row[:, :S], h_banks[t][:])
            else:
                nc.scalar.copy(h_row[:, :S], h_banks[t][:])
            h_rows.append(h_row)
        h_n4s = [ring.tile([P, S], F32, name="h_n4", tag="fetched", bufs=4) for t in range(PACK)]
        st2s = []

        def fetch_h(t):
            nc.vector.tensor_copy(h_n4s[t][:], h_rows[t][:].indirect(n4_t[:]))

        def second_difference(t):
            st2 = keep.tile([P, 2 * S], F32, name="st2", tag="second_window%d" % t)
            nc.vector.tensor_tensor(st2[:, :S], h_banks[t][:], h_n4s[t][:], ALU.subtract)
            st2s.append(st2)

        nc.scalar.activation(h_n4s[2][:], h_rows[2][:].indirect(n4_t[:]), ACT.Copy)
        fetch_h(0)
        fetch_h(1)
        second_difference(0)
        second_difference(1)
        second_difference(2)
        fetch_h(3)
        second_difference(3)
        for t in range(PACK):
            halves = 2 if t == PACK - 1 else 1
            width = S // halves
            for half in range(halves):
                cols = slice(half * width, (half + 1) * width)
                sg = ring.tile([P, width], F32, name="sg", tag="members", bufs=8)
                nc.scalar.activation(
                    sg[:],
                    st2s[t][:].indirect(n5_t[:, half * width // 16 : (half + 1) * width // 16]),
                    ACT.Sigmoid,
                    bias=bias_t[:, t : t + 1],
                    scale=sl_t[:, t : t + 1],
                )
                res = ring.tile([P, width], F32, name="res", tag="members", bufs=8)
                if t < 2:
                    nc.gpsimd.tensor_tensor(res[:], h_rows[t][:, cols], sg[:], ALU.mult)
                else:
                    nc.vector.tensor_tensor(res[:], h_banks[t][:, cols], sg[:], ALU.mult)
                nc.sync.dma_start(out_rows[t][:, cols], res[:])
